import numpy as np
import ml_dtypes


def mxq(x, axis, fmt="e4m3"):
    dtype, down = {"e4m3": (ml_dtypes.float8_e4m3fn, 7), "e5m2": (ml_dtypes.float8_e5m2, 14)}[fmt]
    v = np.moveaxis(np.asarray(x, np.float32).astype(ml_dtypes.bfloat16).astype(np.float64), axis, -1)
    blocks = v.reshape(v.shape[:-1] + (-1, 32))
    amax = np.abs(blocks).max(-1, keepdims=True)
    byte = np.maximum(np.where(amax > 0, np.frexp(amax)[1] - 1 + 127, 0) - down, 1)
    scale = np.exp2(byte - 127.0)
    codes = (blocks / scale).astype(np.float32).astype(dtype).astype(np.float64)
    return np.moveaxis((codes * scale).reshape(v.shape), -1, axis)


WIDE = False


def mx_kscale(k):
    if not WIDE:
        return np.ones(k)
    levels = np.array([10, -10, 5, -5, 0])
    if k % 512:
        return np.exp2(np.random.permutation(np.resize(levels, k // 32))).repeat(32)
    a = np.empty((k // 512, 16))
    for p in range(k // 512):
        a[p, :8] = np.random.permutation(np.resize(levels, 8))
        for g in range(8):
            far = levels[np.abs(levels - a[p, g]) >= 10]
            a[p, g + 8] = far[np.random.randint(len(far))]
    return np.exp2(a.ravel()).repeat(32)


def f64(x):
    return np.asarray(x).astype(np.float64)


def striped(idx):
    return np.tile(np.asarray(idx).reshape(-1, 16).T, (8, 1)).astype(np.uint16)


def unstriped(offs):
    return offs[:16].T.reshape(-1).astype(np.int64)


E2M1 = np.array([0.0, 0.5, 1.0, 1.5, 2.0, 3.0, 4.0, 6.0, -0.0, -0.5, -1.0, -1.5, -2.0, -3.0, -4.0, -6.0])


def pack_weight(w, fmt):
    k, n = w.shape
    w = f64(np.asarray(w, np.float32).astype(ml_dtypes.bfloat16)).reshape(k // 32, 32, n)
    amax = np.abs(w).max(1)
    if fmt == "e4m3":
        byte = np.frexp(amax)[1] - 1 + 127 - 7
    else:
        mant, ex = np.frexp(amax / 6.0)
        byte = np.where(mant > 0.5, ex, ex - 1) + 127
    byte = np.clip(np.where(amax > 0, byte, 1), 1, 254)
    scaled = (w * np.exp2(127.0 - byte)[:, None, :]).reshape(k, n).astype(np.float32)
    by_word = np.ascontiguousarray(scaled.reshape(k // 512, 128, 4, n).transpose(0, 1, 3, 2))
    if fmt == "e4m3":
        words = by_word.astype(ml_dtypes.float8_e4m3fn).view(np.uint8)
    else:
        c = by_word.astype(ml_dtypes.float4_e2m1fn).view(np.uint8) & 0xF
        words = (c[..., 0::2] | (c[..., 1::2] << 4)).reshape(k // 512, 128, 2 * n)
    return np.ascontiguousarray(words), np.ascontiguousarray(byte.astype(np.uint8).reshape(k // 512, 16, n))


def unpack_weight(words, scales, fmt):
    g, _, n = scales.shape
    words = np.ascontiguousarray(words).reshape(g, 128, n, -1)
    if fmt == "e4m3":
        vals = words.view(ml_dtypes.float8_e4m3fn).astype(np.float64)
    else:
        nib = np.empty((g, 128, n, 4), np.uint8)
        nib[..., 0::2] = words & 0xF
        nib[..., 1::2] = words >> 4
        vals = E2M1[nib]
    vals = vals * np.repeat(np.exp2(scales.astype(np.float64) - 127.0), 8, axis=1)[..., None]
    return vals.transpose(0, 1, 3, 2).reshape(g * 512, n)


def sigmoid(v):
    return 1.0 / (1.0 + np.exp(-v))


K, T, J, R, V, N = 512, 2048, 512, 512, 1024, 512


def setup_inputs():
    n = np.random.standard_normal
    idx = np.random.permutation(T)[:J]
    idx2 = np.random.permutation(V)[:J]
    fk = mx_kscale(K)
    fr = mx_kscale(R)
    xtp = pack_weight(n((K, T)) / fk[:, None], "e4m3")
    wap = pack_weight(n((K, R)) * 1 / np.sqrt(K) * fk[:, None] * fr, "e2m1")
    wbp = pack_weight(n((R, N)) * 1 / np.sqrt(R) / fr[:, None], "e4m3")
    wyp = pack_weight(n((K, N)) * 1 / np.sqrt(K) * fk[:, None], "e2m1")
    return {
        "xt_words": xtp[0],
        "xt_scales": xtp[1],
        "wa_words": wap[0],
        "wa_scales": wap[1],
        "tb": (n((R, V))).astype(np.float32),
        "wb_words": wbp[0],
        "wb_scales": wbp[1],
        "wy_words": wyp[0],
        "wy_scales": wyp[1],
        "offs": striped(idx),
        "offs2": striped(idx2),
    }


def reference(xt_words, xt_scales, wa_words, wa_scales, tb, wb_words, wb_scales, wy_words, wy_scales, offs, offs2):
    idx = unstriped(offs)
    idx2 = unstriped(offs2)
    xtu = unpack_weight(xt_words, xt_scales, "e4m3")
    wau = unpack_weight(wa_words, wa_scales, "e2m1")
    wbu = unpack_weight(wb_words, wb_scales, "e4m3")
    wyu = unpack_weight(wy_words, wy_scales, "e2m1")
    xtidxg = xtu[:, idx]
    a = wau.T @ xtidxg
    hid = a * sigmoid(f64(tb)[:, idx2])
    hidq = mxq(hid, 0, "e4m3")
    y = wbu.T @ hidq + wyu.T @ xtidxg
    return y

@@ -1,0 +1,186 @@
+from contextlib import ExitStack
+
+import concourse.mybir as mybir
+
+K, T, J, R, V, N = 512, 2048, 512, 512, 1024, 512
+FLOPS = 2 * J * (K * R + R * N + K * N)
+
+F32 = mybir.dt.float32
+BF16 = mybir.dt.bfloat16
+I32 = mybir.dt.int32
+U32 = mybir.dt.uint32
+U16 = mybir.dt.uint16
+U8 = mybir.dt.uint8
+FP8X4 = mybir.dt.float8_e4m3fn_x4
+FP4X4 = mybir.dt.float4_e2m1fn_x4
+SIGMOID = mybir.ActivationFunctionType.Sigmoid
+MULT = mybir.AluOpType.mult
+
+P = 128
+PACK = 4
+CHUNK = 128
+HALF = 256
+
+
+def load_scale_rows(queue, plane, scales):
+    for q in range(4):
+        queue.dma_start(out=plane[32 * q : 32 * q + 4, :].bitcast(I32), in_=scales[0, 4 * q : 4 * q + 4, :].bitcast(I32))
+
+
+def tile_list_hidden_gated_by_table_kernel(
+    tc, xt_words, xt_scales, wa_words, wa_scales, tb, wb_words, wb_scales, wy_words, wy_scales, offs, offs2, out
+):
+    nc = tc.nc
+    chunks = J // CHUNK
+    with ExitStack() as ctx:
+        sb = ctx.enter_context(tc.tile_pool(name="sb", bufs=1))
+        ps = ctx.enter_context(tc.psum_pool(name="ps", bufs=1))
+
+        tok_list = sb.tile([P, J // 16], U16, name="tok_list")
+        gate_list = sb.tile([P, J // 16], U16, name="gate_list")
+        xt_w = sb.tile([P, T], U32, name="xt_w", align_bytes=64)
+        xt_s = sb.tile([P, T], U8, name="xt_s", align_bytes=64)
+        wa_raw_w = sb.tile([P, 2 * R], U8, name="wa_raw_w", align_bytes=64)
+        wa_raw_s = sb.tile([P, R], U8, name="wa_raw_s", align_bytes=64)
+        wa_w = sb.tile([P, 2 * R], U8, name="wa_w", align_bytes=64)
+        wa_s = sb.tile([P, R], U8, name="wa_s", align_bytes=64)
+        wy_w = sb.tile([P, 2 * N], U8, name="wy_w", align_bytes=64)
+        wy_s = sb.tile([P, N], U8, name="wy_s", align_bytes=64)
+        wb_w = sb.tile([P, N], U32, name="wb_w", align_bytes=64)
+        wb_s = sb.tile([P, N], U8, name="wb_s", align_bytes=64)
+        table = [sb.tile([P, V], F32, name=f"table{t}") for t in range(PACK)]
+        x_w = sb.tile([P, J], U32, name="x_w", align_bytes=64)
+        x_s = sb.tile([P, J], U8, name="x_s", align_bytes=64)
+        gate = [sb.tile([P, 2, J], F32, name=f"gate{u}") for u in range(2)]
+
+        nc.vector.memset(xt_s[:, : T // 2].bitcast(I32), 0)
+        nc.gpsimd.memset(xt_s[:, T // 2 :].bitcast(I32), 0)
+        nc.vector.memset(wa_raw_s[:].bitcast(I32), 0)
+        nc.vector.memset(wy_s[:].bitcast(I32), 0)
+        nc.vector.memset(wb_s[:].bitcast(I32), 0)
+
+        warm = sb.tile([P, 2], F32, name="warm")
+        nc.vector.memset(warm[:, 0:1], 0.0)
+        nc.scalar.activation(warm[:, 1:2], warm[:, 0:1], SIGMOID)
+
+        tb_rows = tb.rearrange("(p t) v -> t p v", t=PACK)
+        nc.sync.dma_start(gate_list[:], offs2)
+        nc.sync.dma_start(tok_list[:], offs)
+        nc.sync.dma_start(out=table[0][:], in_=tb_rows[0])
+        load_scale_rows(nc.sync, xt_s, xt_scales)
+        nc.sync.dma_start(out=xt_w[:].bitcast(I32), in_=xt_words[0].rearrange("p c b -> p (c b)").bitcast(I32))
+        nc.sync.dma_start(out=wa_raw_w[:].bitcast(I32), in_=wa_words[0].bitcast(I32))
+        load_scale_rows(nc.sync, wa_raw_s, wa_scales)
+        nc.sync.dma_start(out=table[1][:], in_=tb_rows[1])
+        nc.sync.dma_start(out=table[2][:], in_=tb_rows[2])
+        load_scale_rows(nc.sync, wy_s, wy_scales)
+        nc.sync.dma_start(out=wy_w[:].bitcast(I32), in_=wy_words[0].bitcast(I32))
+        nc.sync.dma_start(out=table[3][:], in_=tb_rows[3])
+        nc.sync.dma_start(out=wb_w[:].bitcast(I32), in_=wb_words[0].rearrange("p c b -> p (c b)").bitcast(I32))
+        load_scale_rows(nc.sync, wb_s, wb_scales)
+
+        nc.vector.tensor_copy(x_s[:], xt_s[:].indirect(tok_list[:]))
+        nc.vector.tensor_copy(x_w[:, :HALF], xt_w[:].indirect(tok_list[:, : HALF // 16]))
+        nc.vector.tensor_copy(
+            out=wa_w[:].bitcast(U16).rearrange("p (t m) -> p t m", t=PACK),
+            in_=wa_raw_w[:].bitcast(U16).rearrange("p (m t) -> p t m", t=PACK),
+        )
+        nc.vector.tensor_copy(
+            out=wa_s[:].rearrange("p (t m) -> p t m", t=PACK),
+            in_=wa_raw_s[:].rearrange("p (m t) -> p t m", t=PACK),
+        )
+        nc.vector.tensor_copy(x_w[:, HALF:], xt_w[:].indirect(tok_list[:, HALF // 16 :]))
+
+        pre = [[ps.tile([P, 2, HALF], F32, name=f"pre{u}{h}", tag=f"bank{2 * u + h}") for h in range(2)] for u in range(2)]
+        for h in range(2):
+            for u in range(2):
+                cols = slice(h * HALF, (h + 1) * HALF)
+                for i in range(2):
+                    t = 2 * u + i
+                    nc.tensor.matmul_mx(
+                        out=pre[u][h][:, i, :],
+                        lhsT=wa_w[:, 2 * P * t : 2 * P * (t + 1)].bitcast(FP4X4),
+                        lhsT_scale=wa_s[:, P * t : P * (t + 1)],
+                        rhs=x_w[:, cols].bitcast(FP8X4),
+                        rhs_scale=x_s[:, cols],
+                        start=True,
+                        stop=True,
+                    )
+
+        def skip_passes(c, blocks, bank):
+            part = ps.tile([P, len(blocks), CHUNK], F32, name=f"acc{c}_{blocks[0]}", tag=f"bank{bank}")
+            cols = slice(c * CHUNK, (c + 1) * CHUNK)
+            for i, b in enumerate(blocks):
+                nc.tensor.matmul_mx(
+                    out=part[:, i, :],
+                    lhsT=wy_w[:, 2 * P * b : 2 * P * (b + 1)].bitcast(FP4X4),
+                    lhsT_scale=wy_s[:, P * b : P * (b + 1)],
+                    rhs=x_w[:, cols].bitcast(FP8X4),
+                    rhs_scale=x_s[:, cols],
+                    start=(i == 0),
+                    stop=False,
+                )
+            return blocks, part
+
+        acc = [
+            [skip_passes(0, [0, 1, 2, 3], 4)],
+            [skip_passes(1, [0, 1, 2, 3], 5)],
+            [skip_passes(2, [0, 1], 6)],
+            [skip_passes(3, [0, 1], 7)],
+        ]
+
+        for t, width in enumerate([J, HALF, J, CHUNK]):
+            for lo in range(0, J, width):
+                nc.scalar.activation(
+                    gate[t // 2][:, t % 2, lo : lo + width],
+                    table[t][:].indirect(gate_list[:, lo // 16 : (lo + width) // 16]),
+                    SIGMOID,
+                )
+
+        hid = [sb.tile([P, CHUNK, PACK], BF16, name=f"hid{c}", align_bytes=64) for c in range(chunks)]
+        hid_w = [sb.tile([P, CHUNK], U32, name=f"hid_w{c}", align_bytes=64) for c in range(chunks)]
+        hid_s = [sb.tile([P, CHUNK], U8, name=f"hid_s{c}", align_bytes=64) for c in range(chunks)]
+        out_rows = out.rearrange("(b p) j -> p b j", p=P)
+
+        def gate_pair(u, c):
+            h, lo = divmod(c * CHUNK, HALF)
+            nc.vector.tensor_tensor(
+                out=hid[c][:, :, 2 * u : 2 * u + 2],
+                in0=pre[u][h][:, :, lo : lo + CHUNK].rearrange("p i j -> p j i"),
+                in1=gate[u][:, :, c * CHUNK : (c + 1) * CHUNK].rearrange("p i j -> p j i"),
+                op=MULT,
+            )
+
+        def finish(c):
+            nc.vector.quantize_mx(
+                out=hid_w[c][:].bitcast(FP8X4), scales=hid_s[c][:], in_=hid[c][:].rearrange("p j t -> p (j t)")
+            )
+            for k, (blocks, part) in enumerate(acc[c]):
+                for i, b in enumerate(blocks):
+                    nc.tensor.matmul_mx(
+                        out=part[:, i, :],
+                        lhsT=wb_w[:, P * b : P * (b + 1)].bitcast(FP8X4),
+                        lhsT_scale=wb_s[:, P * b : P * (b + 1)],
+                        rhs=hid_w[c][:].bitcast(FP8X4),
+                        rhs_scale=hid_s[c][:],
+                        start=False,
+                        stop=(i == len(blocks) - 1),
+                    )
+                res = sb.tile([P, len(blocks), CHUNK], F32, name=f"res{c}_{k}")
+                if k == 0:
+                    nc.scalar.copy(res[:], part[:])
+                else:
+                    nc.vector.tensor_copy(res[:], part[:])
+                nc.sync.dma_start(
+                    out=out_rows[:, blocks[0] : blocks[-1] + 1, c * CHUNK : (c + 1) * CHUNK], in_=res[:]
+                )
+
+        for c in range(chunks):
+            gate_pair(0, c)
+        acc[2].append(skip_passes(2, [2, 3], 0))
+        acc[3].append(skip_passes(3, [2, 3], 1))
+        gate_pair(1, 0)
+        for c in range(chunks):
+            if c + 1 < chunks:
+                gate_pair(1, c + 1)
+            finish(c)

@@ -23,8 +23,8 @@ HALF = 256
 
 
 def load_scale_rows(queue, plane, scales):
-    for q in range(4):
-        queue.dma_start(out=plane[32 * q : 32 * q + 4, :].bitcast(I32), in_=scales[0, 4 * q : 4 * q + 4, :].bitcast(I32))
+    for r in range(4):
+        queue.dma_start(out=plane[r:P:32, :].bitcast(I32), in_=scales[0, r:16:4, :].bitcast(I32))
 
 
 def tile_list_hidden_gated_by_table_kernel(
@@ -64,12 +64,12 @@ def tile_list_hidden_gated_by_table_kernel(
         nc.scalar.activation(warm[:, 1:2], warm[:, 0:1], SIGMOID)
 
         tb_rows = tb.rearrange("(p t) v -> t p v", t=PACK)
-        nc.sync.dma_start(gate_list[:], offs2)
-        nc.sync.dma_start(tok_list[:], offs)
         nc.sync.dma_start(out=table[0][:], in_=tb_rows[0])
+        nc.sync.dma_start(tok_list[:], offs)
+        nc.sync.dma_start(out=wa_raw_w[:].bitcast(I32), in_=wa_words[0].bitcast(I32))
         load_scale_rows(nc.sync, xt_s, xt_scales)
         nc.sync.dma_start(out=xt_w[:].bitcast(I32), in_=xt_words[0].rearrange("p c b -> p (c b)").bitcast(I32))
-        nc.sync.dma_start(out=wa_raw_w[:].bitcast(I32), in_=wa_words[0].bitcast(I32))
+        nc.sync.dma_start(gate_list[:], offs2)
         load_scale_rows(nc.sync, wa_raw_s, wa_scales)
         nc.sync.dma_start(out=table[1][:], in_=tb_rows[1])
         nc.sync.dma_start(out=table[2][:], in_=tb_rows[2])
@@ -123,10 +123,8 @@ def tile_list_hidden_gated_by_table_kernel(
             return blocks, part
 
         acc = [
-            [skip_passes(0, [0, 1, 2, 3], 4)],
-            [skip_passes(1, [0, 1, 2, 3], 5)],
-            [skip_passes(2, [0, 1], 6)],
-            [skip_passes(3, [0, 1], 7)],
+            [skip_passes(0, [0, 1], 4), skip_passes(0, [2, 3], 5)],
+            [skip_passes(1, [0, 1], 6), skip_passes(1, [2, 3], 7)],
         ]
 
         for t, width in enumerate([J, HALF, J, CHUNK]):
@@ -167,7 +165,7 @@ def tile_list_hidden_gated_by_table_kernel(
                         stop=(i == len(blocks) - 1),
                     )
                 res = sb.tile([P, len(blocks), CHUNK], F32, name=f"res{c}_{k}")
-                if k == 0:
+                if c < 2 or (c, k) == (3, 0):
                     nc.scalar.copy(res[:], part[:])
                 else:
                     nc.vector.tensor_copy(res[:], part[:])
@@ -177,10 +175,14 @@ def tile_list_hidden_gated_by_table_kernel(
 
         for c in range(chunks):
             gate_pair(0, c)
-        acc[2].append(skip_passes(2, [2, 3], 0))
-        acc[3].append(skip_passes(3, [2, 3], 1))
+        acc.append([skip_passes(2, [0, 1, 2, 3], 0)])
+        acc.append([skip_passes(3, [0, 1], 1)])
         gate_pair(1, 0)
-        for c in range(chunks):
-            if c + 1 < chunks:
-                gate_pair(1, c + 1)
-            finish(c)
+        finish(0)
+        gate_pair(1, 1)
+        acc[3].append(skip_passes(3, [2, 3], 2))
+        gate_pair(1, 2)
+        finish(1)
+        gate_pair(1, 3)
+        finish(2)
+        finish(3)

@@ -18,13 +18,15 @@ MULT = mybir.AluOpType.mult
 
 P = 128
 PACK = 4
+GROUP = 16
+QUADRANT = 32
 CHUNK = 128
 HALF = 256
 
 
-def load_scale_rows(queue, plane, scales):
-    for r in range(4):
-        queue.dma_start(out=plane[r:P:32, :].bitcast(I32), in_=scales[0, r:16:4, :].bitcast(I32))
+def load_scale_rows(nc, plane, scales):
+    for first in range(4):
+        nc.sync.dma_start(out=plane[first:P:QUADRANT, :].bitcast(I32), in_=scales[0, first:16:4, :].bitcast(I32))
 
 
 def tile_list_hidden_gated_by_table_kernel(
@@ -36,8 +38,8 @@ def tile_list_hidden_gated_by_table_kernel(
         sb = ctx.enter_context(tc.tile_pool(name="sb", bufs=1))
         ps = ctx.enter_context(tc.psum_pool(name="ps", bufs=1))
 
-        tok_list = sb.tile([P, J // 16], U16, name="tok_list")
-        gate_list = sb.tile([P, J // 16], U16, name="gate_list")
+        tok_list = sb.tile([P, J // GROUP], U16, name="tok_list")
+        gate_list = sb.tile([P, J // GROUP], U16, name="gate_list")
         xt_w = sb.tile([P, T], U32, name="xt_w", align_bytes=64)
         xt_s = sb.tile([P, T], U8, name="xt_s", align_bytes=64)
         wa_raw_w = sb.tile([P, 2 * R], U8, name="wa_raw_w", align_bytes=64)
@@ -59,28 +61,24 @@ def tile_list_hidden_gated_by_table_kernel(
         nc.vector.memset(wy_s[:].bitcast(I32), 0)
         nc.vector.memset(wb_s[:].bitcast(I32), 0)
 
-        warm = sb.tile([P, 2], F32, name="warm")
-        nc.vector.memset(warm[:, 0:1], 0.0)
-        nc.scalar.activation(warm[:, 1:2], warm[:, 0:1], SIGMOID)
-
         tb_rows = tb.rearrange("(p t) v -> t p v", t=PACK)
         nc.sync.dma_start(out=table[0][:], in_=tb_rows[0])
-        nc.sync.dma_start(tok_list[:], offs)
-        nc.sync.dma_start(out=wa_raw_w[:].bitcast(I32), in_=wa_words[0].bitcast(I32))
-        load_scale_rows(nc.sync, xt_s, xt_scales)
-        nc.sync.dma_start(out=xt_w[:].bitcast(I32), in_=xt_words[0].rearrange("p c b -> p (c b)").bitcast(I32))
         nc.sync.dma_start(gate_list[:], offs2)
-        load_scale_rows(nc.sync, wa_raw_s, wa_scales)
+        nc.sync.dma_start(tok_list[:], offs)
+        load_scale_rows(nc, xt_s, xt_scales)
+        nc.sync.dma_start(out=xt_w[:].bitcast(I32), in_=xt_words[0].rearrange("p c b -> p (c b)").bitcast(I32))
+        nc.sync.dma_start(out=wa_raw_w[:].bitcast(I32), in_=wa_words[0].bitcast(I32))
+        load_scale_rows(nc, wa_raw_s, wa_scales)
         nc.sync.dma_start(out=table[1][:], in_=tb_rows[1])
         nc.sync.dma_start(out=table[2][:], in_=tb_rows[2])
-        load_scale_rows(nc.sync, wy_s, wy_scales)
+        load_scale_rows(nc, wy_s, wy_scales)
         nc.sync.dma_start(out=wy_w[:].bitcast(I32), in_=wy_words[0].bitcast(I32))
         nc.sync.dma_start(out=table[3][:], in_=tb_rows[3])
         nc.sync.dma_start(out=wb_w[:].bitcast(I32), in_=wb_words[0].rearrange("p c b -> p (c b)").bitcast(I32))
-        load_scale_rows(nc.sync, wb_s, wb_scales)
+        load_scale_rows(nc, wb_s, wb_scales)
 
         nc.vector.tensor_copy(x_s[:], xt_s[:].indirect(tok_list[:]))
-        nc.vector.tensor_copy(x_w[:, :HALF], xt_w[:].indirect(tok_list[:, : HALF // 16]))
+        nc.vector.tensor_copy(x_w[:, :HALF], xt_w[:].indirect(tok_list[:, : HALF // GROUP]))
         nc.vector.tensor_copy(
             out=wa_w[:].bitcast(U16).rearrange("p (t m) -> p t m", t=PACK),
             in_=wa_raw_w[:].bitcast(U16).rearrange("p (m t) -> p t m", t=PACK),
@@ -89,9 +87,11 @@ def tile_list_hidden_gated_by_table_kernel(
             out=wa_s[:].rearrange("p (t m) -> p t m", t=PACK),
             in_=wa_raw_s[:].rearrange("p (m t) -> p t m", t=PACK),
         )
-        nc.vector.tensor_copy(x_w[:, HALF:], xt_w[:].indirect(tok_list[:, HALF // 16 :]))
+        nc.vector.tensor_copy(x_w[:, HALF:], xt_w[:].indirect(tok_list[:, HALF // GROUP :]))
 
-        pre = [[ps.tile([P, 2, HALF], F32, name=f"pre{u}{h}", tag=f"bank{2 * u + h}") for h in range(2)] for u in range(2)]
+        pre = [
+            [ps.tile([P, 2, HALF], F32, name=f"pre{u}{h}", tag=f"bank{2 * u + h}") for h in range(2)] for u in range(2)
+        ]
         for h in range(2):
             for u in range(2):
                 cols = slice(h * HALF, (h + 1) * HALF)
@@ -107,31 +107,59 @@ def tile_list_hidden_gated_by_table_kernel(
                         stop=True,
                     )
 
-        def skip_passes(c, blocks, bank):
-            part = ps.tile([P, len(blocks), CHUNK], F32, name=f"acc{c}_{blocks[0]}", tag=f"bank{bank}")
+        def skip_pass(part, i, b, c, start, stop):
             cols = slice(c * CHUNK, (c + 1) * CHUNK)
+            nc.tensor.matmul_mx(
+                out=part[:, i, :],
+                lhsT=wy_w[:, 2 * P * b : 2 * P * (b + 1)].bitcast(FP4X4),
+                lhsT_scale=wy_s[:, P * b : P * (b + 1)],
+                rhs=x_w[:, cols].bitcast(FP8X4),
+                rhs_scale=x_s[:, cols],
+                start=start,
+                stop=stop,
+            )
+
+        def hidden_pass(part, i, b, c, start, stop):
+            nc.tensor.matmul_mx(
+                out=part[:, i, :],
+                lhsT=wb_w[:, P * b : P * (b + 1)].bitcast(FP8X4),
+                lhsT_scale=wb_s[:, P * b : P * (b + 1)],
+                rhs=hid_w[c][:].bitcast(FP8X4),
+                rhs_scale=hid_s[c][:],
+                start=start,
+                stop=stop,
+            )
+
+        def open_piece(c, blocks, bank):
+            part = ps.tile([P, len(blocks), CHUNK], F32, name=f"acc{c}_{blocks[0]}", tag=f"bank{bank}")
             for i, b in enumerate(blocks):
-                nc.tensor.matmul_mx(
-                    out=part[:, i, :],
-                    lhsT=wy_w[:, 2 * P * b : 2 * P * (b + 1)].bitcast(FP4X4),
-                    lhsT_scale=wy_s[:, P * b : P * (b + 1)],
-                    rhs=x_w[:, cols].bitcast(FP8X4),
-                    rhs_scale=x_s[:, cols],
-                    start=(i == 0),
-                    stop=False,
-                )
+                skip_pass(part, i, b, c, i == 0, False)
+            return blocks, part
+
+        def close_piece(c, piece):
+            blocks, part = piece
+            for i, b in enumerate(blocks):
+                hidden_pass(part, i, b, c, False, i == len(blocks) - 1)
+
+        def late_piece(c, blocks, bank):
+            part = ps.tile([P, len(blocks), CHUNK], F32, name=f"acc{c}_{blocks[0]}", tag=f"bank{bank}")
+            for i, b in enumerate(blocks):
+                hidden_pass(part, i, b, c, i == 0, False)
+            for i, b in enumerate(blocks):
+                skip_pass(part, i, b, c, False, i == len(blocks) - 1)
             return blocks, part
 
         acc = [
-            [skip_passes(0, [0, 1], 4), skip_passes(0, [2, 3], 5)],
-            [skip_passes(1, [0, 1], 6), skip_passes(1, [2, 3], 7)],
+            [open_piece(0, [0, 1], 4), open_piece(0, [2, 3], 5)],
+            [open_piece(1, [0, 1], 6)],
+            [open_piece(2, [0, 1], 7)],
         ]
 
         for t, width in enumerate([J, HALF, J, CHUNK]):
             for lo in range(0, J, width):
                 nc.scalar.activation(
                     gate[t // 2][:, t % 2, lo : lo + width],
-                    table[t][:].indirect(gate_list[:, lo // 16 : (lo + width) // 16]),
+                    table[t][:].indirect(gate_list[:, lo // GROUP : (lo + width) // GROUP]),
                     SIGMOID,
                 )
 
@@ -143,9 +171,9 @@ def tile_list_hidden_gated_by_table_kernel(
         def gate_pair(u, c):
             h, lo = divmod(c * CHUNK, HALF)
             nc.vector.tensor_tensor(
-                out=hid[c][:, :, 2 * u : 2 * u + 2],
-                in0=pre[u][h][:, :, lo : lo + CHUNK].rearrange("p i j -> p j i"),
-                in1=gate[u][:, :, c * CHUNK : (c + 1) * CHUNK].rearrange("p i j -> p j i"),
+                out=hid[c][:, :, 2 * u : 2 * u + 2].rearrange("p (j e) i -> p j i e", e=2),
+                in0=pre[u][h][:, :, lo : lo + CHUNK].rearrange("p i (j e) -> p j i e", e=2),
+                in1=gate[u][:, :, c * CHUNK : (c + 1) * CHUNK].rearrange("p i (j e) -> p j i e", e=2),
                 op=MULT,
             )
 
@@ -153,36 +181,33 @@ def tile_list_hidden_gated_by_table_kernel(
             nc.vector.quantize_mx(
                 out=hid_w[c][:].bitcast(FP8X4), scales=hid_s[c][:], in_=hid[c][:].rearrange("p j t -> p (j t)")
             )
-            for k, (blocks, part) in enumerate(acc[c]):
-                for i, b in enumerate(blocks):
-                    nc.tensor.matmul_mx(
-                        out=part[:, i, :],
-                        lhsT=wb_w[:, P * b : P * (b + 1)].bitcast(FP8X4),
-                        lhsT_scale=wb_s[:, P * b : P * (b + 1)],
-                        rhs=hid_w[c][:].bitcast(FP8X4),
-                        rhs_scale=hid_s[c][:],
-                        start=False,
-                        stop=(i == len(blocks) - 1),
-                    )
-                res = sb.tile([P, len(blocks), CHUNK], F32, name=f"res{c}_{k}")
-                if c < 2 or (c, k) == (3, 0):
-                    nc.scalar.copy(res[:], part[:])
-                else:
-                    nc.vector.tensor_copy(res[:], part[:])
-                nc.sync.dma_start(
-                    out=out_rows[:, blocks[0] : blocks[-1] + 1, c * CHUNK : (c + 1) * CHUNK], in_=res[:]
-                )
+            for piece in acc[c]:
+                close_piece(c, piece)
+
+        def store(c, which):
+            blocks, part = acc[c][which]
+            res = sb.tile([P, len(blocks), CHUNK], F32, name=f"res{c}_{which}")
+            if which == 0 or c == 0:
+                nc.scalar.copy(res[:], part[:])
+            else:
+                nc.vector.tensor_copy(res[:], part[:])
+            nc.sync.dma_start(out=out_rows[:, blocks[0] : blocks[-1] + 1, c * CHUNK : (c + 1) * CHUNK], in_=res[:])
 
         for c in range(chunks):
             gate_pair(0, c)
-        acc.append([skip_passes(2, [0, 1, 2, 3], 0)])
-        acc.append([skip_passes(3, [0, 1], 1)])
+        acc[2].append(open_piece(2, [2, 3], 0))
+        acc.append([open_piece(3, [0, 1, 2], 1)])
+
         gate_pair(1, 0)
-        finish(0)
         gate_pair(1, 1)
-        acc[3].append(skip_passes(3, [2, 3], 2))
+        finish(0)
         gate_pair(1, 2)
         finish(1)
+        acc[1].append(late_piece(1, [2, 3], 2))
         gate_pair(1, 3)
         finish(2)
         finish(3)
+        acc[3].append(late_piece(3, [3], 3))
+        for c in range(chunks):
+            for which in range(len(acc[c])):
+                store(c, which)

from contextlib import ExitStack

import concourse.mybir as mybir

K, T, J, R, V, N = 512, 2048, 512, 512, 1024, 512
FLOPS = 2 * J * (K * R + R * N + K * N)

F32 = mybir.dt.float32
BF16 = mybir.dt.bfloat16
I32 = mybir.dt.int32
U32 = mybir.dt.uint32
U16 = mybir.dt.uint16
U8 = mybir.dt.uint8
FP8X4 = mybir.dt.float8_e4m3fn_x4
FP4X4 = mybir.dt.float4_e2m1fn_x4
SIGMOID = mybir.ActivationFunctionType.Sigmoid
MULT = mybir.AluOpType.mult

P = 128
PACK = 4
GROUP = 16
QUADRANT = 32
CHUNK = 128
HALF = 256


def load_scale_rows(nc, plane, scales):
    for first in range(4):
        nc.sync.dma_start(out=plane[first:P:QUADRANT, :].bitcast(I32), in_=scales[0, first:16:4, :].bitcast(I32))


def tile_list_hidden_gated_by_table_kernel(
    tc, xt_words, xt_scales, wa_words, wa_scales, tb, wb_words, wb_scales, wy_words, wy_scales, offs, offs2, out
):
    nc = tc.nc
    chunks = J // CHUNK
    with ExitStack() as ctx:
        sb = ctx.enter_context(tc.tile_pool(name="sb", bufs=1))
        ps = ctx.enter_context(tc.psum_pool(name="ps", bufs=1))

        tok_list = sb.tile([P, J // GROUP], U16, name="tok_list")
        gate_list = sb.tile([P, J // GROUP], U16, name="gate_list")
        xt_w = sb.tile([P, T], U32, name="xt_w", align_bytes=64)
        xt_s = sb.tile([P, T], U8, name="xt_s", align_bytes=64)
        wa_raw_w = sb.tile([P, 2 * R], U8, name="wa_raw_w", align_bytes=64)
        wa_raw_s = sb.tile([P, R], U8, name="wa_raw_s", align_bytes=64)
        wa_w = sb.tile([P, 2 * R], U8, name="wa_w", align_bytes=64)
        wa_s = sb.tile([P, R], U8, name="wa_s", align_bytes=64)
        wy_w = sb.tile([P, 2 * N], U8, name="wy_w", align_bytes=64)
        wy_s = sb.tile([P, N], U8, name="wy_s", align_bytes=64)
        wb_w = sb.tile([P, N], U32, name="wb_w", align_bytes=64)
        wb_s = sb.tile([P, N], U8, name="wb_s", align_bytes=64)
        table = [sb.tile([P, V], F32, name=f"table{t}") for t in range(PACK)]
        x_w = sb.tile([P, J], U32, name="x_w", align_bytes=64)
        x_s = sb.tile([P, J], U8, name="x_s", align_bytes=64)
        gate = [sb.tile([P, 2, J], F32, name=f"gate{u}") for u in range(2)]

        nc.vector.memset(xt_s[:, : T // 2].bitcast(I32), 0)
        nc.gpsimd.memset(xt_s[:, T // 2 :].bitcast(I32), 0)
        nc.vector.memset(wa_raw_s[:].bitcast(I32), 0)
        nc.vector.memset(wy_s[:].bitcast(I32), 0)
        nc.vector.memset(wb_s[:].bitcast(I32), 0)

        tb_rows = tb.rearrange("(p t) v -> t p v", t=PACK)
        nc.sync.dma_start(out=table[0][:], in_=tb_rows[0])
        nc.sync.dma_start(gate_list[:], offs2)
        nc.sync.dma_start(tok_list[:], offs)
        load_scale_rows(nc, xt_s, xt_scales)
        nc.sync.dma_start(out=xt_w[:].bitcast(I32), in_=xt_words[0].rearrange("p c b -> p (c b)").bitcast(I32))
        nc.sync.dma_start(out=wa_raw_w[:].bitcast(I32), in_=wa_words[0].bitcast(I32))
        load_scale_rows(nc, wa_raw_s, wa_scales)
        nc.sync.dma_start(out=table[1][:], in_=tb_rows[1])
        nc.sync.dma_start(out=table[2][:], in_=tb_rows[2])
        load_scale_rows(nc, wy_s, wy_scales)
        nc.sync.dma_start(out=wy_w[:].bitcast(I32), in_=wy_words[0].bitcast(I32))
        nc.sync.dma_start(out=table[3][:], in_=tb_rows[3])
        nc.sync.dma_start(out=wb_w[:].bitcast(I32), in_=wb_words[0].rearrange("p c b -> p (c b)").bitcast(I32))
        load_scale_rows(nc, wb_s, wb_scales)

        nc.vector.tensor_copy(x_s[:], xt_s[:].indirect(tok_list[:]))
        nc.vector.tensor_copy(x_w[:, :HALF], xt_w[:].indirect(tok_list[:, : HALF // GROUP]))
        nc.vector.tensor_copy(
            out=wa_w[:].bitcast(U16).rearrange("p (t m) -> p t m", t=PACK),
            in_=wa_raw_w[:].bitcast(U16).rearrange("p (m t) -> p t m", t=PACK),
        )
        nc.vector.tensor_copy(
            out=wa_s[:].rearrange("p (t m) -> p t m", t=PACK),
            in_=wa_raw_s[:].rearrange("p (m t) -> p t m", t=PACK),
        )
        nc.vector.tensor_copy(x_w[:, HALF:], xt_w[:].indirect(tok_list[:, HALF // GROUP :]))

        pre = [
            [ps.tile([P, 2, HALF], F32, name=f"pre{u}{h}", tag=f"bank{2 * u + h}") for h in range(2)] for u in range(2)
        ]
        for h in range(2):
            for u in range(2):
                cols = slice(h * HALF, (h + 1) * HALF)
                for i in range(2):
                    t = 2 * u + i
                    nc.tensor.matmul_mx(
                        out=pre[u][h][:, i, :],
                        lhsT=wa_w[:, 2 * P * t : 2 * P * (t + 1)].bitcast(FP4X4),
                        lhsT_scale=wa_s[:, P * t : P * (t + 1)],
                        rhs=x_w[:, cols].bitcast(FP8X4),
                        rhs_scale=x_s[:, cols],
                        start=True,
                        stop=True,
                    )

        def skip_pass(part, i, b, c, start, stop):
            cols = slice(c * CHUNK, (c + 1) * CHUNK)
            nc.tensor.matmul_mx(
                out=part[:, i, :],
                lhsT=wy_w[:, 2 * P * b : 2 * P * (b + 1)].bitcast(FP4X4),
                lhsT_scale=wy_s[:, P * b : P * (b + 1)],
                rhs=x_w[:, cols].bitcast(FP8X4),
                rhs_scale=x_s[:, cols],
                start=start,
                stop=stop,
            )

        def hidden_pass(part, i, b, c, start, stop):
            nc.tensor.matmul_mx(
                out=part[:, i, :],
                lhsT=wb_w[:, P * b : P * (b + 1)].bitcast(FP8X4),
                lhsT_scale=wb_s[:, P * b : P * (b + 1)],
                rhs=hid_w[c][:].bitcast(FP8X4),
                rhs_scale=hid_s[c][:],
                start=start,
                stop=stop,
            )

        def open_piece(c, blocks, bank):
            part = ps.tile([P, len(blocks), CHUNK], F32, name=f"acc{c}_{blocks[0]}", tag=f"bank{bank}")
            for i, b in enumerate(blocks):
                skip_pass(part, i, b, c, i == 0, False)
            return blocks, part

        def close_piece(c, piece):
            blocks, part = piece
            for i, b in enumerate(blocks):
                hidden_pass(part, i, b, c, False, i == len(blocks) - 1)

        def late_piece(c, blocks, bank):
            part = ps.tile([P, len(blocks), CHUNK], F32, name=f"acc{c}_{blocks[0]}", tag=f"bank{bank}")
            for i, b in enumerate(blocks):
                hidden_pass(part, i, b, c, i == 0, False)
            for i, b in enumerate(blocks):
                skip_pass(part, i, b, c, False, i == len(blocks) - 1)
            return blocks, part

        acc = [
            [open_piece(0, [0, 1], 4), open_piece(0, [2, 3], 5)],
            [open_piece(1, [0, 1], 6)],
            [open_piece(2, [0, 1], 7)],
        ]

        for t, width in enumerate([J, HALF, J, CHUNK]):
            for lo in range(0, J, width):
                nc.scalar.activation(
                    gate[t // 2][:, t % 2, lo : lo + width],
                    table[t][:].indirect(gate_list[:, lo // GROUP : (lo + width) // GROUP]),
                    SIGMOID,
                )

        hid = [sb.tile([P, CHUNK, PACK], BF16, name=f"hid{c}", align_bytes=64) for c in range(chunks)]
        hid_w = [sb.tile([P, CHUNK], U32, name=f"hid_w{c}", align_bytes=64) for c in range(chunks)]
        hid_s = [sb.tile([P, CHUNK], U8, name=f"hid_s{c}", align_bytes=64) for c in range(chunks)]
        out_rows = out.rearrange("(b p) j -> p b j", p=P)

        def gate_pair(u, c):
            h, lo = divmod(c * CHUNK, HALF)
            nc.vector.tensor_tensor(
                out=hid[c][:, :, 2 * u : 2 * u + 2].rearrange("p (j e) i -> p j i e", e=2),
                in0=pre[u][h][:, :, lo : lo + CHUNK].rearrange("p i (j e) -> p j i e", e=2),
                in1=gate[u][:, :, c * CHUNK : (c + 1) * CHUNK].rearrange("p i (j e) -> p j i e", e=2),
                op=MULT,
            )

        def finish(c):
            nc.vector.quantize_mx(
                out=hid_w[c][:].bitcast(FP8X4), scales=hid_s[c][:], in_=hid[c][:].rearrange("p j t -> p (j t)")
            )
            for piece in acc[c]:
                close_piece(c, piece)

        def store(c, which):
            blocks, part = acc[c][which]
            res = sb.tile([P, len(blocks), CHUNK], F32, name=f"res{c}_{which}")
            if which == 0 or c == 0:
                nc.scalar.copy(res[:], part[:])
            else:
                nc.vector.tensor_copy(res[:], part[:])
            nc.sync.dma_start(out=out_rows[:, blocks[0] : blocks[-1] + 1, c * CHUNK : (c + 1) * CHUNK], in_=res[:])

        for c in range(chunks):
            gate_pair(0, c)
        acc[2].append(open_piece(2, [2, 3], 0))
        acc.append([open_piece(3, [0, 1, 2], 1)])

        gate_pair(1, 0)
        gate_pair(1, 1)
        finish(0)
        gate_pair(1, 2)
        finish(1)
        acc[1].append(late_piece(1, [2, 3], 2))
        gate_pair(1, 3)
        finish(2)
        finish(3)
        acc[3].append(late_piece(3, [3], 3))
        for c in range(chunks):
            for which in range(len(acc[c])):
                store(c, which)
